import numpy as np
import ml_dtypes


def mxq(x, axis, fmt="e4m3"):
    dtype, down = {"e4m3": (ml_dtypes.float8_e4m3fn, 7), "e5m2": (ml_dtypes.float8_e5m2, 14)}[fmt]
    v = np.moveaxis(np.asarray(x, np.float32).astype(ml_dtypes.bfloat16).astype(np.float64), axis, -1)
    blocks = v.reshape(v.shape[:-1] + (-1, 32))
    amax = np.abs(blocks).max(-1, keepdims=True)
    byte = np.maximum(np.where(amax > 0, np.frexp(amax)[1] - 1 + 127, 0) - down, 1)
    scale = np.exp2(byte - 127.0)
    codes = (blocks / scale).astype(np.float32).astype(dtype).astype(np.float64)
    return np.moveaxis((codes * scale).reshape(v.shape), -1, axis)


WIDE = False


def mx_kscale(k):
    if not WIDE:
        return np.ones(k)
    levels = np.array([10, -10, 5, -5, 0])
    if k % 512:
        return np.exp2(np.random.permutation(np.resize(levels, k // 32))).repeat(32)
    a = np.empty((k // 512, 16))
    for p in range(k // 512):
        a[p, :8] = np.random.permutation(np.resize(levels, 8))
        for g in range(8):
            far = levels[np.abs(levels - a[p, g]) >= 10]
            a[p, g + 8] = far[np.random.randint(len(far))]
    return np.exp2(a.ravel()).repeat(32)


def f64(x):
    return np.asarray(x).astype(np.float64)


def striped(idx):
    return np.tile(idx.reshape(-1, 16).T, (8, 1)).astype(np.uint16)


def unstriped(offs):
    return offs[:16].T.reshape(-1).astype(np.int64)


def striped8(idx):
    return np.concatenate([x.reshape(-1, 16).T for x in idx]).astype(np.uint16)


def runs(offs, k):
    lists = np.stack([offs[16 * r : 16 * r + 16].T.reshape(-1) for r in range(8)]).astype(np.int64)
    return lists[np.arange(k) % 512 // 64]


def pack_weight(w):
    k, n = w.shape
    w = f64(np.asarray(w, np.float32).astype(ml_dtypes.bfloat16)).reshape(k // 32, 32, n)
    amax = np.abs(w).max(1)
    byte = np.clip(np.where(amax > 0, np.frexp(amax)[1] - 1 + 127 - 7, 1), 1, 254)
    scaled = (w * np.exp2(127.0 - byte)[:, None, :]).reshape(k, n).astype(np.float32)
    words = np.ascontiguousarray(scaled.reshape(k // 512, 128, 4, n).transpose(0, 1, 3, 2)).astype(ml_dtypes.float8_e4m3fn).view(np.uint8)
    return words, np.ascontiguousarray(byte.astype(np.uint8).reshape(k // 512, 16, n))


def unpack_weight(words, scales):
    g, p, n, _ = words.shape
    vals = np.ascontiguousarray(words).view(ml_dtypes.float8_e4m3fn).astype(np.float64) * np.repeat(np.exp2(scales.astype(np.float64) - 127.0), 8, axis=1)[..., None]
    return vals.transpose(0, 1, 3, 2).reshape(g * 512, n)


K, T, S, N, G, H, U = 512, 2048, 512, 512, 2048, 512, 1024


def setup_inputs():
    n = np.random.standard_normal
    s = mx_kscale(K)[:, None]
    u = mx_kscale(H)
    packed_xT = pack_weight(n((K, T)) * s)
    packed_dT = pack_weight(n((K, G)) / s)
    return {
        "x_words": packed_xT[0],
        "x_scales": packed_xT[1],
        "d_words": packed_dT[0],
        "d_scales": packed_dT[1],
        "old": n((H, U)).astype(np.float32),
        "gn": (np.random.uniform(0.5, 1.5, (H, 1)) * u[:, None]).astype(np.float32),
        "w1": (n((H, N)) / np.sqrt(H) / u[:, None]).astype(np.float32),
        "offs": striped(np.random.permutation(T)[:S]),
        "kidx": striped8(np.random.randint(0, G, (8, H))),
        "slot": striped8(np.stack([np.random.permutation(U)[:S] for _ in range(8)])),
    }


def reference(x_words, x_scales, d_words, d_scales, old, gn, w1, offs, kidx, slot):
    d_kidx = unpack_weight(d_words, d_scales)[np.arange(K)[:, None], runs(kidx, K)]
    xq = unpack_weight(x_words, x_scales)[:, unstriped(offs)]
    s = 0.0625 * (d_kidx.T @ xq)
    nw = np.maximum(s, 0.5 * (f64(old)[np.arange(H)[:, None], runs(slot, H)]))
    pg = f64(old).copy()
    pg[np.arange(H)[:, None], runs(slot, H)] = nw
    z = f64(gn) * pg
    return mxq(f64(w1), 0, "e4m3").T @ mxq(z, 0, "e4m3")

@@ -1,0 +1,195 @@
+from contextlib import ExitStack
+
+import concourse.mybir as mybir
+
+K, T, S, N, G, H, U = 512, 2048, 512, 512, 2048, 512, 1024
+FLOPS = 2 * K * H * S + 2 * H * N * U
+
+F32 = mybir.dt.float32
+BF16 = mybir.dt.bfloat16
+I32 = mybir.dt.int32
+U32 = mybir.dt.uint32
+U16 = mybir.dt.uint16
+U8 = mybir.dt.uint8
+FP8X4 = mybir.dt.float8_e4m3fn_x4
+ALU = mybir.AluOpType
+COPY = mybir.ActivationFunctionType.Copy
+
+P = 128
+PACK = 4
+BANK = 512
+ORDER = (2, 0, 1, 3)
+CHUNKS = (256, 256, 256, 256)
+SCALAR_CHUNK = 1
+
+
+def tile_picked_scorepage_none_p_kernel(
+    tc, x_words, x_scales, d_words, d_scales, old, gn, w1, offs, kidx, slot, out
+):
+    nc = tc.nc
+    with ExitStack() as ctx:
+        keep = ctx.enter_context(tc.tile_pool(name="keep", bufs=1))
+        psum = ctx.enter_context(tc.psum_pool(name="psum", bufs=8))
+
+        kidx_sb = keep.tile([P, H // 16], U16, name="kidx_sb")
+        offs_sb = keep.tile([P, S // 16], U16, name="offs_sb")
+        slot_sb = keep.tile([P, S // 16], U16, name="slot_sb")
+        d_tab = keep.tile([P, G], U32, name="d_tab", tag="room_a", align_bytes=64)
+        x_tab = keep.tile([P, T], U32, name="x_tab", tag="room_b", align_bytes=64)
+        ds_tab = keep.tile([P, G], U8, name="ds_tab", tag="room_c", align_bytes=64)
+        xs_tab = keep.tile([P, T], U8, name="xs_tab", tag="room_d", align_bytes=64)
+        halves = keep.tile([P, S], F32, name="halves", tag="room_g", align_bytes=64)
+        page = {}
+        old_rows = old.rearrange("(p t) u -> t p u", t=PACK)
+
+        def load_page(t, room):
+            page[t] = keep.tile([P, U], F32, name=f"page{t}", tag=room, align_bytes=64)
+            nc.sync.dma_start(page[t][:], old_rows[t])
+
+        nc.gpsimd.memset(ds_tab[:].bitcast(I32), 0)
+        nc.vector.memset(xs_tab[:].bitcast(I32), 0)
+        nc.vector.memset(halves[:], 0.5)
+
+        nc.sync.dma_start(kidx_sb[:], kidx)
+        nc.scalar.dma_start(ds_tab[0:P:8, :].bitcast(I32), d_scales[0].bitcast(I32))
+        nc.sync.dma_start(offs_sb[:], offs)
+        nc.scalar.dma_start(xs_tab[0:P:8, :].bitcast(I32), x_scales[0].bitcast(I32))
+        nc.sync.dma_start(slot_sb[:], slot)
+        gn_sb = keep.tile([P, PACK], F32, name="gn_sb")
+        nc.sync.dma_start(gn_sb[:], gn.rearrange("(p t) o -> p (t o)", t=PACK))
+        nc.sync.dma_start(d_tab[:].bitcast(I32), d_words[0].rearrange("p n t -> p (n t)").bitcast(I32))
+        nc.sync.dma_start(x_tab[:].bitcast(I32), x_words[0].rearrange("p n t -> p (n t)").bitcast(I32))
+        load_page(ORDER[0], "room_f")
+
+        ds_got = keep.tile([P, H], U8, name="ds_got", align_bytes=64)
+        planes = keep.tile([P, H + S], U8, name="planes", align_bytes=64)
+        d_dealt = keep.tile([P, H], U32, name="d_dealt", align_bytes=64)
+
+        nc.vector.tensor_copy(ds_got[:], ds_tab[:].indirect(kidx_sb[:]))
+        xs_got = keep.tile([P, S], U8, name="xs_got", tag="room_c", align_bytes=64)
+        nc.vector.tensor_copy(xs_got[:], xs_tab[:].indirect(offs_sb[:]))
+        nc.vector.tensor_copy(
+            planes[:, :H].rearrange("p (t m) -> p t m", t=PACK), ds_got[:].rearrange("p (m t) -> p t m", t=PACK)
+        )
+        nc.vector.tensor_copy(planes[:, H:].bitcast(I32), xs_got[:].bitcast(I32))
+        for j in range(1, 4):
+            nc.scalar.dma_start(planes[j:P:32, :].bitcast(I32), planes[8 * j : P : 32, :].bitcast(I32))
+        d_got = keep.tile([P, H], U32, name="d_got", tag="room_d", align_bytes=64)
+        nc.vector.tensor_copy(d_got[:], d_tab[:].indirect(kidx_sb[:]))
+        nc.vector.tensor_copy(
+            d_dealt[:].rearrange("p (t m) -> p t m", t=PACK), d_got[:].rearrange("p (m t) -> p t m", t=PACK)
+        )
+        load_page(ORDER[1], "room_c")
+        load_page(ORDER[2], "room_d")
+        x_got = keep.tile([P, S], U32, name="x_got", tag="room_a", align_bytes=64)
+        nc.vector.tensor_copy(x_got[:], x_tab[:].indirect(offs_sb[:]))
+        w_raw = keep.tile([P, PACK, N], F32, name="w_raw", tag="room_b", align_bytes=64)
+        nc.sync.dma_start(w_raw[:], w1.rearrange("(p t) n -> p t n", t=PACK))
+        held = [keep.tile([P, S], F32, name=f"held{t}") for t in range(PACK)]
+
+        def fetch_held(t):
+            nc.vector.tensor_copy(held[t][:], page[t][:].indirect(slot_sb[:]))
+
+        fetch_held(ORDER[0])
+
+        score = {}
+        for t in ORDER:
+            score[t] = psum.tile([P, S], F32, name=f"score{t}", tag="bank")
+            cols = slice(t * P, (t + 1) * P)
+            nc.tensor.matmul_mx(
+                out=score[t][:],
+                lhsT=d_dealt[:, cols].bitcast(FP8X4),
+                lhsT_scale=planes[:, cols],
+                rhs=x_got[:].bitcast(FP8X4),
+                rhs_scale=planes[:, H:],
+                start=True,
+                stop=True,
+            )
+
+        load_page(ORDER[3], "room_a")
+        starts = [sum(CHUNKS[:c]) for c in range(len(CHUNKS))]
+        z = [keep.tile([P, w, PACK], BF16, name=f"z{c}", align_bytes=64) for c, w in enumerate(CHUNKS)]
+        w_bf = keep.tile([P, N, PACK], BF16, name="w_bf", align_bytes=64)
+        w_sc = keep.tile([P, N], U8, name="w_sc", align_bytes=64)
+
+        for i, t in enumerate(ORDER):
+            if i + 1 < PACK:
+                fetch_held(ORDER[i + 1])
+            new = keep.tile([P, S], F32, name=f"new{t}", tag="room_f" if i + 1 == PACK else f"new{t}", align_bytes=64)
+            nc.vector.scalar_tensor_tensor(new[:], score[t][:], 0.125, held[t][:], ALU.mult, ALU.max)
+            nc.vector.tensor_tensor(page[t][:].indirect(slot_sb[:]), new[:], halves[:], ALU.mult)
+            if i + 1 < PACK:
+                for c, w in enumerate(CHUNKS):
+                    nc.scalar.activation(
+                        z[c][:, :, t], page[t][:, starts[c] : starts[c] + w], COPY, scale=gn_sb[:, t : t + 1]
+                    )
+            if i == 0:
+                nc.scalar.copy(w_bf[:], w_raw[:].rearrange("p t n -> p n t"))
+
+        t = ORDER[-1]
+        w_codes = keep.tile([P, N], U32, name="w_codes", tag="room_g", align_bytes=64)
+        z_codes = [keep.tile([P, w], U32, name=f"z_codes{c}", align_bytes=64) for c, w in enumerate(CHUNKS)]
+        z_sc = [keep.tile([P, w], U8, name=f"z_sc{c}", align_bytes=64) for c, w in enumerate(CHUNKS)]
+
+        def weigh_last(c):
+            cols = slice(starts[c], starts[c] + CHUNKS[c])
+            if c == SCALAR_CHUNK:
+                nc.scalar.activation(z[c][:, :, t], page[t][:, cols], COPY, scale=gn_sb[:, t : t + 1])
+            else:
+                nc.vector.tensor_scalar(z[c][:, :, t], page[t][:, cols], gn_sb[:, t : t + 1], None, ALU.mult)
+
+        def quantise_w(a, b):
+            nc.vector.quantize_mx(
+                out=w_codes[:, a:b].bitcast(FP8X4),
+                scales=w_sc[:, a:b],
+                in_=w_bf[:, a:b, :].rearrange("p n t -> p (n t)"),
+            )
+
+        def quantise_z(c):
+            nc.vector.quantize_mx(
+                out=z_codes[c][:].bitcast(FP8X4), scales=z_sc[c][:], in_=z[c][:].rearrange("p n t -> p (n t)")
+            )
+
+        def multiply(c, m0, per_bank, on_vector):
+            w = CHUNKS[c]
+            acc = psum.tile([P, per_bank, w], F32, name=f"acc{c}_{m0}", tag="bank")
+            for a in range(per_bank):
+                cols = slice((m0 + a) * P, (m0 + a + 1) * P)
+                nc.tensor.matmul_mx(
+                    out=acc[:, a, :],
+                    lhsT=w_codes[:, cols].bitcast(FP8X4),
+                    lhsT_scale=w_sc[:, cols],
+                    rhs=z_codes[c][:].bitcast(FP8X4),
+                    rhs_scale=z_sc[c][:],
+                    start=True,
+                    stop=True,
+                )
+            res = keep.tile([P, per_bank, w], F32, name=f"res{c}_{m0}")
+            if on_vector:
+                nc.vector.tensor_copy(res[:], acc[:])
+            else:
+                nc.scalar.copy(res[:], acc[:])
+            nc.sync.dma_start(
+                out[m0 * P : (m0 + per_bank) * P, starts[c] : starts[c] + w].rearrange("(a p) n -> p a n", p=P),
+                res[:],
+            )
+
+        weigh_last(0)
+        weigh_last(1)
+        quantise_w(0, P)
+        quantise_z(0)
+        quantise_w(P, 2 * P)
+        quantise_w(2 * P, N)
+        quantise_z(1)
+        weigh_last(2)
+        weigh_last(3)
+        quantise_z(2)
+        quantise_z(3)
+        multiply(0, 0, 1, False)
+        multiply(0, 1, 1, False)
+        multiply(0, 2, 2, False)
+        multiply(1, 0, 2, False)
+        multiply(1, 2, 2, False)
+        for c in (2, 3):
+            multiply(c, 0, 2, False)
+            multiply(c, 2, 2, True)

@@ -1,6 +1,7 @@
 from contextlib import ExitStack
 
 import concourse.mybir as mybir
+from concourse.masks import make_identity
 
 K, T, S, N, G, H, U = 512, 2048, 512, 512, 2048, 512, 1024
 FLOPS = 2 * K * H * S + 2 * H * N * U
@@ -18,9 +19,10 @@ COPY = mybir.ActivationFunctionType.Copy
 P = 128
 PACK = 4
 BANK = 512
-ORDER = (2, 0, 1, 3)
+ORDER = (0, 2, 3, 1)
 CHUNKS = (256, 256, 256, 256)
-SCALAR_CHUNK = 1
+PIECE = 256
+SCALAR_CHUNKS = (1, 2)
 
 
 def tile_picked_scorepage_none_p_kernel(
@@ -34,11 +36,13 @@ def tile_picked_scorepage_none_p_kernel(
         kidx_sb = keep.tile([P, H // 16], U16, name="kidx_sb")
         offs_sb = keep.tile([P, S // 16], U16, name="offs_sb")
         slot_sb = keep.tile([P, S // 16], U16, name="slot_sb")
+        gn_sb = keep.tile([P, PACK], F32, name="gn_sb")
         d_tab = keep.tile([P, G], U32, name="d_tab", tag="room_a", align_bytes=64)
         x_tab = keep.tile([P, T], U32, name="x_tab", tag="room_b", align_bytes=64)
-        ds_tab = keep.tile([P, G], U8, name="ds_tab", tag="room_c", align_bytes=64)
-        xs_tab = keep.tile([P, T], U8, name="xs_tab", tag="room_d", align_bytes=64)
-        halves = keep.tile([P, S], F32, name="halves", tag="room_g", align_bytes=64)
+        ds_tab = keep.tile([P, G], U8, name="ds_tab", align_bytes=64)
+        xs_tab = keep.tile([P, T], U8, name="xs_tab", align_bytes=64)
+        planes = keep.tile([P, H + S], U8, name="planes", align_bytes=64)
+        ident = keep.tile([P, P], F32, name="ident")
         page = {}
         old_rows = old.rearrange("(p t) u -> t p u", t=PACK)
 
@@ -46,78 +50,82 @@ def tile_picked_scorepage_none_p_kernel(
             page[t] = keep.tile([P, U], F32, name=f"page{t}", tag=room, align_bytes=64)
             nc.sync.dma_start(page[t][:], old_rows[t])
 
-        nc.gpsimd.memset(ds_tab[:].bitcast(I32), 0)
-        nc.vector.memset(xs_tab[:].bitcast(I32), 0)
-        nc.vector.memset(halves[:], 0.5)
+        nc.vector.memset(ds_tab[:].bitcast(I32), 0)
+        nc.vector.memset(xs_tab[:, : T // 2].bitcast(I32), 0)
+        nc.gpsimd.memset(xs_tab[:, T // 2 :].bitcast(I32), 0)
+        nc.vector.memset(planes[:].bitcast(I32), 0)
+        nc.vector.memset(ident[:], 0.0)
+        make_identity(nc, ident[:], nomemset=True)
 
         nc.sync.dma_start(kidx_sb[:], kidx)
-        nc.scalar.dma_start(ds_tab[0:P:8, :].bitcast(I32), d_scales[0].bitcast(I32))
         nc.sync.dma_start(offs_sb[:], offs)
-        nc.scalar.dma_start(xs_tab[0:P:8, :].bitcast(I32), x_scales[0].bitcast(I32))
         nc.sync.dma_start(slot_sb[:], slot)
-        gn_sb = keep.tile([P, PACK], F32, name="gn_sb")
         nc.sync.dma_start(gn_sb[:], gn.rearrange("(p t) o -> p (t o)", t=PACK))
-        nc.sync.dma_start(d_tab[:].bitcast(I32), d_words[0].rearrange("p n t -> p (n t)").bitcast(I32))
+        nc.sync.dma_start(ds_tab[0:P:8, :].bitcast(I32), d_scales[0].bitcast(I32))
+        d_src = d_words[0].rearrange("p n t -> p (n t)").bitcast(I32)
+        nc.sync.dma_start(d_tab[:, :PIECE].bitcast(I32), d_src[:, :PIECE])
+        nc.sync.dma_start(xs_tab[0:P:8, :].bitcast(I32), x_scales[0].bitcast(I32))
+        nc.sync.dma_start(d_tab[:, PIECE:].bitcast(I32), d_src[:, PIECE:])
         nc.sync.dma_start(x_tab[:].bitcast(I32), x_words[0].rearrange("p n t -> p (n t)").bitcast(I32))
         load_page(ORDER[0], "room_f")
 
-        ds_got = keep.tile([P, H], U8, name="ds_got", align_bytes=64)
-        planes = keep.tile([P, H + S], U8, name="planes", align_bytes=64)
-        d_dealt = keep.tile([P, H], U32, name="d_dealt", align_bytes=64)
-
-        nc.vector.tensor_copy(ds_got[:], ds_tab[:].indirect(kidx_sb[:]))
-        xs_got = keep.tile([P, S], U8, name="xs_got", tag="room_c", align_bytes=64)
-        nc.vector.tensor_copy(xs_got[:], xs_tab[:].indirect(offs_sb[:]))
-        nc.vector.tensor_copy(
-            planes[:, :H].rearrange("p (t m) -> p t m", t=PACK), ds_got[:].rearrange("p (m t) -> p t m", t=PACK)
-        )
-        nc.vector.tensor_copy(planes[:, H:].bitcast(I32), xs_got[:].bitcast(I32))
-        for j in range(1, 4):
-            nc.scalar.dma_start(planes[j:P:32, :].bitcast(I32), planes[8 * j : P : 32, :].bitcast(I32))
+        sc_got = keep.tile([P, H + S], U8, name="sc_got", tag="room_c", align_bytes=64)
         d_got = keep.tile([P, H], U32, name="d_got", tag="room_d", align_bytes=64)
-        nc.vector.tensor_copy(d_got[:], d_tab[:].indirect(kidx_sb[:]))
-        nc.vector.tensor_copy(
-            d_dealt[:].rearrange("p (t m) -> p t m", t=PACK), d_got[:].rearrange("p (m t) -> p t m", t=PACK)
-        )
-        load_page(ORDER[1], "room_c")
-        load_page(ORDER[2], "room_d")
-        x_got = keep.tile([P, S], U32, name="x_got", tag="room_a", align_bytes=64)
-        nc.vector.tensor_copy(x_got[:], x_tab[:].indirect(offs_sb[:]))
-        w_raw = keep.tile([P, PACK, N], F32, name="w_raw", tag="room_b", align_bytes=64)
-        nc.sync.dma_start(w_raw[:], w1.rearrange("(p t) n -> p t n", t=PACK))
+        x_got = keep.tile([P, S], U32, name="x_got", align_bytes=64)
         held = [keep.tile([P, S], F32, name=f"held{t}") for t in range(PACK)]
 
         def fetch_held(t):
             nc.vector.tensor_copy(held[t][:], page[t][:].indirect(slot_sb[:]))
 
-        fetch_held(ORDER[0])
-
-        score = {}
+        nc.vector.tensor_copy(sc_got[:, :H], ds_tab[:].indirect(kidx_sb[:]))
+        nc.vector.tensor_copy(sc_got[:, H:], xs_tab[:].indirect(offs_sb[:]))
+        for j in range(4):
+            nc.scalar.dma_start(planes[j:P:32, :].bitcast(I32), sc_got[8 * j : P : 32, :].bitcast(I32))
+        nc.vector.tensor_copy(d_got[:], d_tab[:].indirect(kidx_sb[:]))
+        load_page(ORDER[1], "room_a")
+        load_page(ORDER[2], "room_c")
+        nc.vector.tensor_copy(x_got[:], x_tab[:].indirect(offs_sb[:]))
+        load_page(ORDER[3], "room_b")
         for t in ORDER:
-            score[t] = psum.tile([P, S], F32, name=f"score{t}", tag="bank")
-            cols = slice(t * P, (t + 1) * P)
+            fetch_held(t)
+
+        raw = []
+        for b in range(S // P):
+            bank = psum.tile([P, H], F32, name=f"raw{b}", tag="bank")
+            cols = slice(b * P, (b + 1) * P)
             nc.tensor.matmul_mx(
-                out=score[t][:],
-                lhsT=d_dealt[:, cols].bitcast(FP8X4),
-                lhsT_scale=planes[:, cols],
-                rhs=x_got[:].bitcast(FP8X4),
-                rhs_scale=planes[:, H:],
+                out=bank[:],
+                lhsT=x_got[:, cols].bitcast(FP8X4),
+                lhsT_scale=planes[:, H + b * P : H + (b + 1) * P],
+                rhs=d_got[:].bitcast(FP8X4),
+                rhs_scale=planes[:, :H],
                 start=True,
                 stop=True,
             )
+            raw.append(bank[:].rearrange("p (m t) -> p t m", t=PACK))
+        w_raw = keep.tile([P, PACK, N], F32, name="w_raw", tag="room_d", align_bytes=64)
+        nc.sync.dma_start(w_raw[:], w1.rearrange("(p t) n -> p t n", t=PACK))
+        dealt = [keep.tile([P, PACK, P], F32, name=f"dealt{b}") for b in range(S // P)]
+        score = {t: psum.tile([P, S], F32, name=f"score{t}", tag="bank") for t in ORDER}
 
-        load_page(ORDER[3], "room_a")
+        def turn(t):
+            for b in range(S // P):
+                nc.tensor.transpose(score[t][:, b * P : (b + 1) * P], dealt[b][:, t, :], ident[:])
+
+        for b in range(S // P):
+            nc.scalar.activation(dealt[b][:], raw[b], COPY, scale=0.0625)
+        for t in ORDER:
+            turn(t)
+
         starts = [sum(CHUNKS[:c]) for c in range(len(CHUNKS))]
         z = [keep.tile([P, w, PACK], BF16, name=f"z{c}", align_bytes=64) for c, w in enumerate(CHUNKS)]
         w_bf = keep.tile([P, N, PACK], BF16, name="w_bf", align_bytes=64)
         w_sc = keep.tile([P, N], U8, name="w_sc", align_bytes=64)
 
         for i, t in enumerate(ORDER):
-            if i + 1 < PACK:
-                fetch_held(ORDER[i + 1])
             new = keep.tile([P, S], F32, name=f"new{t}", tag="room_f" if i + 1 == PACK else f"new{t}", align_bytes=64)
-            nc.vector.scalar_tensor_tensor(new[:], score[t][:], 0.125, held[t][:], ALU.mult, ALU.max)
-            nc.vector.tensor_tensor(page[t][:].indirect(slot_sb[:]), new[:], halves[:], ALU.mult)
+            nc.vector.scalar_tensor_tensor(new[:], held[t][:], 0.5, score[t][:], ALU.mult, ALU.max)
+            nc.vector.tensor_copy(page[t][:].indirect(slot_sb[:]), new[:])
             if i + 1 < PACK:
                 for c, w in enumerate(CHUNKS):
                     nc.scalar.activation(
@@ -127,13 +135,13 @@ def tile_picked_scorepage_none_p_kernel(
                 nc.scalar.copy(w_bf[:], w_raw[:].rearrange("p t n -> p n t"))
 
         t = ORDER[-1]
-        w_codes = keep.tile([P, N], U32, name="w_codes", tag="room_g", align_bytes=64)
+        w_codes = keep.tile([P, N], U32, name="w_codes", tag="room_f", align_bytes=64)
         z_codes = [keep.tile([P, w], U32, name=f"z_codes{c}", align_bytes=64) for c, w in enumerate(CHUNKS)]
         z_sc = [keep.tile([P, w], U8, name=f"z_sc{c}", align_bytes=64) for c, w in enumerate(CHUNKS)]
 
         def weigh_last(c):
             cols = slice(starts[c], starts[c] + CHUNKS[c])
-            if c == SCALAR_CHUNK:
+            if c in SCALAR_CHUNKS:
                 nc.scalar.activation(z[c][:, :, t], page[t][:, cols], COPY, scale=gn_sb[:, t : t + 1])
             else:
                 nc.vector.tensor_scalar(z[c][:, :, t], page[t][:, cols], gn_sb[:, t : t + 1], None, ALU.mult)
@@ -176,20 +184,18 @@ def tile_picked_scorepage_none_p_kernel(
 
         weigh_last(0)
         weigh_last(1)
+        weigh_last(2)
         quantise_w(0, P)
         quantise_z(0)
         quantise_w(P, 2 * P)
         quantise_w(2 * P, N)
         quantise_z(1)
-        weigh_last(2)
         weigh_last(3)
         quantise_z(2)
         quantise_z(3)
         multiply(0, 0, 1, False)
         multiply(0, 1, 1, False)
         multiply(0, 2, 2, False)
-        multiply(1, 0, 2, False)
-        multiply(1, 2, 2, False)
-        for c in (2, 3):
+        for c in (1, 2, 3):
             multiply(c, 0, 2, False)
             multiply(c, 2, 2, True)

@@ -22,7 +22,7 @@ BANK = 512
 ORDER = (0, 2, 3, 1)
 CHUNKS = (256, 256, 256, 256)
 PIECE = 256
-SCALAR_CHUNKS = (1, 2)
+SCALAR_CHUNKS = (1,)
 
 
 def tile_picked_scorepage_none_p_kernel(
@@ -118,8 +118,8 @@ def tile_picked_scorepage_none_p_kernel(
             turn(t)
 
         starts = [sum(CHUNKS[:c]) for c in range(len(CHUNKS))]
-        z = [keep.tile([P, w, PACK], BF16, name=f"z{c}", align_bytes=64) for c, w in enumerate(CHUNKS)]
-        w_bf = keep.tile([P, N, PACK], BF16, name="w_bf", align_bytes=64)
+        z = [keep.tile([P, w, PACK], BF16, name=f"z{c}", tag=f"room_z{c}", align_bytes=64) for c, w in enumerate(CHUNKS)]
+        w_bf = keep.tile([P, N, PACK], BF16, name="w_bf", tag="room_w", align_bytes=64)
         w_sc = keep.tile([P, N], U8, name="w_sc", align_bytes=64)
 
         for i, t in enumerate(ORDER):
@@ -135,20 +135,22 @@ def tile_picked_scorepage_none_p_kernel(
                 nc.scalar.copy(w_bf[:], w_raw[:].rearrange("p t n -> p n t"))
 
         t = ORDER[-1]
-        w_codes = keep.tile([P, N], U32, name="w_codes", tag="room_f", align_bytes=64)
+        w_codes = {}
         z_codes = [keep.tile([P, w], U32, name=f"z_codes{c}", align_bytes=64) for c, w in enumerate(CHUNKS)]
         z_sc = [keep.tile([P, w], U8, name=f"z_sc{c}", align_bytes=64) for c, w in enumerate(CHUNKS)]
 
-        def weigh_last(c):
+        def weigh_last(c, weight):
             cols = slice(starts[c], starts[c] + CHUNKS[c])
             if c in SCALAR_CHUNKS:
-                nc.scalar.activation(z[c][:, :, t], page[t][:, cols], COPY, scale=gn_sb[:, t : t + 1])
+                nc.scalar.activation(z[c][:, :, t], page[t][:, cols], COPY, scale=weight)
             else:
-                nc.vector.tensor_scalar(z[c][:, :, t], page[t][:, cols], gn_sb[:, t : t + 1], None, ALU.mult)
+                nc.vector.tensor_scalar(z[c][:, :, t], page[t][:, cols], weight, None, ALU.mult)
 
-        def quantise_w(a, b):
+        def quantise_w(codes, a, b):
+            for m in range(a // P, b // P):
+                w_codes[m] = codes[:, m * P - a : (m + 1) * P - a]
             nc.vector.quantize_mx(
-                out=w_codes[:, a:b].bitcast(FP8X4),
+                out=codes.bitcast(FP8X4),
                 scales=w_sc[:, a:b],
                 in_=w_bf[:, a:b, :].rearrange("p n t -> p (n t)"),
             )
@@ -165,7 +167,7 @@ def tile_picked_scorepage_none_p_kernel(
                 cols = slice((m0 + a) * P, (m0 + a + 1) * P)
                 nc.tensor.matmul_mx(
                     out=acc[:, a, :],
-                    lhsT=w_codes[:, cols].bitcast(FP8X4),
+                    lhsT=w_codes[m0 + a].bitcast(FP8X4),
                     lhsT_scale=w_sc[:, cols],
                     rhs=z_codes[c][:].bitcast(FP8X4),
                     rhs_scale=z_sc[c][:],
@@ -182,15 +184,19 @@ def tile_picked_scorepage_none_p_kernel(
                 res[:],
             )
 
-        weigh_last(0)
-        weigh_last(1)
-        weigh_last(2)
-        quantise_w(0, P)
+        weigh_last(0, gn_sb[:, t : t + 1])
+        weigh_last(1, gn_sb[:, t : t + 1])
+        w_first = keep.tile([P, P], U32, name="w_first", tag="room_f", align_bytes=64)
+        quantise_w(w_first[:], 0, P)
         quantise_z(0)
-        quantise_w(P, 2 * P)
-        quantise_w(2 * P, N)
+        w_rest = keep.tile([P, N - P], U32, name="w_rest", tag="room_z0", align_bytes=64)
+        quantise_w(w_rest[:, :P], P, 2 * P)
+        quantise_w(w_rest[:, P:], 2 * P, N)
         quantise_z(1)
-        weigh_last(3)
+        gn_last = keep.tile([P, 1], F32, name="gn_last", tag="room_w", align_bytes=64)
+        nc.vector.tensor_copy(gn_last[:], gn_sb[:, t : t + 1])
+        weigh_last(2, gn_last[:])
+        weigh_last(3, gn_last[:])
         quantise_z(2)
         quantise_z(3)
         multiply(0, 0, 1, False)
@@ -198,4 +204,4 @@ def tile_picked_scorepage_none_p_kernel(
         multiply(0, 2, 2, False)
         for c in (1, 2, 3):
             multiply(c, 0, 2, False)
-            multiply(c, 2, 2, True)
+            multiply(c, 2, 2, c >= 2)

@@ -22,7 +22,7 @@ BANK = 512
 ORDER = (0, 2, 3, 1)
 CHUNKS = (256, 256, 256, 256)
 PIECE = 256
-SCALAR_CHUNKS = (1,)
+SCALAR_CHUNKS = (0, 1)
 
 
 def tile_picked_scorepage_none_p_kernel(
@@ -67,7 +67,7 @@ def tile_picked_scorepage_none_p_kernel(
         nc.sync.dma_start(xs_tab[0:P:8, :].bitcast(I32), x_scales[0].bitcast(I32))
         nc.sync.dma_start(d_tab[:, PIECE:].bitcast(I32), d_src[:, PIECE:])
         nc.sync.dma_start(x_tab[:].bitcast(I32), x_words[0].rearrange("p n t -> p (n t)").bitcast(I32))
-        load_page(ORDER[0], "room_f")
+        load_page(ORDER[0], "page_first")
 
         sc_got = keep.tile([P, H + S], U8, name="sc_got", tag="room_c", align_bytes=64)
         d_got = keep.tile([P, H], U32, name="d_got", tag="room_d", align_bytes=64)
@@ -119,23 +119,30 @@ def tile_picked_scorepage_none_p_kernel(
 
         starts = [sum(CHUNKS[:c]) for c in range(len(CHUNKS))]
         z = [keep.tile([P, w, PACK], BF16, name=f"z{c}", tag=f"room_z{c}", align_bytes=64) for c, w in enumerate(CHUNKS)]
-        w_bf = keep.tile([P, N, PACK], BF16, name="w_bf", tag="room_w", align_bytes=64)
+        w_bf = keep.tile([P, N, PACK], BF16, name="w_bf", align_bytes=64)
         w_sc = keep.tile([P, N], U8, name="w_sc", align_bytes=64)
 
+        new = {}
+
+        def take_larger(t):
+            new[t] = keep.tile([P, S], F32, name=f"new{t}", tag=f"room_new{t}", align_bytes=64)
+            nc.vector.scalar_tensor_tensor(new[t][:], held[t][:], 0.5, score[t][:], ALU.mult, ALU.max)
+
+        nc.scalar.copy(w_bf[:], w_raw[:].rearrange("p t n -> p n t"))
+        gn_use = keep.tile([P, PACK], F32, name="gn_use", tag="room_d", align_bytes=64)
+        nc.scalar.copy(gn_use[:], gn_sb[:])
+        take_larger(ORDER[0])
         for i, t in enumerate(ORDER):
-            new = keep.tile([P, S], F32, name=f"new{t}", tag="room_f" if i + 1 == PACK else f"new{t}", align_bytes=64)
-            nc.vector.scalar_tensor_tensor(new[:], held[t][:], 0.5, score[t][:], ALU.mult, ALU.max)
-            nc.vector.tensor_copy(page[t][:].indirect(slot_sb[:]), new[:])
+            if i + 1 < PACK:
+                take_larger(ORDER[i + 1])
+            nc.vector.tensor_copy(page[t][:].indirect(slot_sb[:]), new[t][:])
             if i + 1 < PACK:
                 for c, w in enumerate(CHUNKS):
                     nc.scalar.activation(
-                        z[c][:, :, t], page[t][:, starts[c] : starts[c] + w], COPY, scale=gn_sb[:, t : t + 1]
+                        z[c][:, :, t], page[t][:, starts[c] : starts[c] + w], COPY, scale=gn_use[:, t : t + 1]
                     )
-            if i == 0:
-                nc.scalar.copy(w_bf[:], w_raw[:].rearrange("p t n -> p n t"))
 
         t = ORDER[-1]
-        w_codes = {}
         z_codes = [keep.tile([P, w], U32, name=f"z_codes{c}", align_bytes=64) for c, w in enumerate(CHUNKS)]
         z_sc = [keep.tile([P, w], U8, name=f"z_sc{c}", align_bytes=64) for c, w in enumerate(CHUNKS)]
 
@@ -145,15 +152,6 @@ def tile_picked_scorepage_none_p_kernel(
                 nc.scalar.activation(z[c][:, :, t], page[t][:, cols], COPY, scale=weight)
             else:
                 nc.vector.tensor_scalar(z[c][:, :, t], page[t][:, cols], weight, None, ALU.mult)
-
-        def quantise_w(codes, a, b):
-            for m in range(a // P, b // P):
-                w_codes[m] = codes[:, m * P - a : (m + 1) * P - a]
-            nc.vector.quantize_mx(
-                out=codes.bitcast(FP8X4),
-                scales=w_sc[:, a:b],
-                in_=w_bf[:, a:b, :].rearrange("p n t -> p (n t)"),
-            )
 
         def quantise_z(c):
             nc.vector.quantize_mx(
@@ -167,7 +165,7 @@ def tile_picked_scorepage_none_p_kernel(
                 cols = slice((m0 + a) * P, (m0 + a + 1) * P)
                 nc.tensor.matmul_mx(
                     out=acc[:, a, :],
-                    lhsT=w_codes[m0 + a].bitcast(FP8X4),
+                    lhsT=w_codes[:, cols].bitcast(FP8X4),
                     lhsT_scale=w_sc[:, cols],
                     rhs=z_codes[c][:].bitcast(FP8X4),
                     rhs_scale=z_sc[c][:],
@@ -184,18 +182,15 @@ def tile_picked_scorepage_none_p_kernel(
                 res[:],
             )
 
-        weigh_last(0, gn_sb[:, t : t + 1])
-        weigh_last(1, gn_sb[:, t : t + 1])
-        w_first = keep.tile([P, P], U32, name="w_first", tag="room_f", align_bytes=64)
-        quantise_w(w_first[:], 0, P)
+        weigh_last(0, gn_use[:, t : t + 1])
+        weigh_last(1, gn_use[:, t : t + 1])
+        w_codes = keep.tile([P, N], U32, name="w_codes", tag=f"room_new{t}", align_bytes=64)
+        nc.vector.quantize_mx(out=w_codes[:].bitcast(FP8X4), scales=w_sc[:], in_=w_bf[:].rearrange("p n t -> p (n t)"))
         quantise_z(0)
-        w_rest = keep.tile([P, N - P], U32, name="w_rest", tag="room_z0", align_bytes=64)
-        quantise_w(w_rest[:, :P], P, 2 * P)
-        quantise_w(w_rest[:, P:], 2 * P, N)
-        quantise_z(1)
-        gn_last = keep.tile([P, 1], F32, name="gn_last", tag="room_w", align_bytes=64)
+        gn_last = keep.tile([P, 1], F32, name="gn_last", tag="room_z0", align_bytes=64)
         nc.vector.tensor_copy(gn_last[:], gn_sb[:, t : t + 1])
         weigh_last(2, gn_last[:])
+        quantise_z(1)
         weigh_last(3, gn_last[:])
         quantise_z(2)
         quantise_z(3)

@@ -18,11 +18,17 @@ COPY = mybir.ActivationFunctionType.Copy
 
 P = 128
 PACK = 4
-BANK = 512
-ORDER = (0, 2, 3, 1)
-CHUNKS = (256, 256, 256, 256)
-PIECE = 256
-SCALAR_CHUNKS = (0, 1)
+GROUP = 16
+BLOCK_ROWS = 8
+QUADRANT = 32
+PSUM_BANKS = 8
+SCORE_SCALE = 0.0625
+OLD_SCALE = 0.5
+
+PLANES = (0, 2, 3, 1)
+CHUNK = 256
+CHUNKS = U // CHUNK
+D_AHEAD = 512
 
 
 def tile_picked_scorepage_none_p_kernel(
@@ -31,172 +37,161 @@ def tile_picked_scorepage_none_p_kernel(
     nc = tc.nc
     with ExitStack() as ctx:
         keep = ctx.enter_context(tc.tile_pool(name="keep", bufs=1))
-        psum = ctx.enter_context(tc.psum_pool(name="psum", bufs=8))
+        psum = ctx.enter_context(tc.psum_pool(name="psum", bufs=PSUM_BANKS))
 
-        kidx_sb = keep.tile([P, H // 16], U16, name="kidx_sb")
-        offs_sb = keep.tile([P, S // 16], U16, name="offs_sb")
-        slot_sb = keep.tile([P, S // 16], U16, name="slot_sb")
+        kidx_sb = keep.tile([P, H // GROUP], U16, name="kidx_sb")
+        offs_sb = keep.tile([P, S // GROUP], U16, name="offs_sb")
+        slot_sb = keep.tile([P, S // GROUP], U16, name="slot_sb")
         gn_sb = keep.tile([P, PACK], F32, name="gn_sb")
-        d_tab = keep.tile([P, G], U32, name="d_tab", tag="room_a", align_bytes=64)
-        x_tab = keep.tile([P, T], U32, name="x_tab", tag="room_b", align_bytes=64)
-        ds_tab = keep.tile([P, G], U8, name="ds_tab", align_bytes=64)
-        xs_tab = keep.tile([P, T], U8, name="xs_tab", align_bytes=64)
-        planes = keep.tile([P, H + S], U8, name="planes", align_bytes=64)
-        ident = keep.tile([P, P], F32, name="ident")
+        d_table = keep.tile([P, G], U32, name="d_table", tag="d_table", align_bytes=64)
+        x_table = keep.tile([P, T], U32, name="x_table", tag="x_table", align_bytes=64)
+        d_scale_table = keep.tile([P, G], U8, name="d_scale_table", align_bytes=64)
+        x_scale_table = keep.tile([P, T], U8, name="x_scale_table", align_bytes=64)
+        scales = keep.tile([P, H + S], U8, name="scales", align_bytes=64)
+        identity = keep.tile([P, P], F32, name="identity")
         page = {}
-        old_rows = old.rearrange("(p t) u -> t p u", t=PACK)
+        old_planes = old.rearrange("(p t) u -> t p u", t=PACK)
 
-        def load_page(t, room):
-            page[t] = keep.tile([P, U], F32, name=f"page{t}", tag=room, align_bytes=64)
-            nc.sync.dma_start(page[t][:], old_rows[t])
+        def load_page(t, tag):
+            page[t] = keep.tile([P, U], F32, name=f"page{t}", tag=tag, align_bytes=64)
+            nc.sync.dma_start(page[t][:], old_planes[t])
 
-        nc.vector.memset(ds_tab[:].bitcast(I32), 0)
-        nc.vector.memset(xs_tab[:, : T // 2].bitcast(I32), 0)
-        nc.gpsimd.memset(xs_tab[:, T // 2 :].bitcast(I32), 0)
-        nc.vector.memset(planes[:].bitcast(I32), 0)
-        nc.vector.memset(ident[:], 0.0)
-        make_identity(nc, ident[:], nomemset=True)
+        nc.vector.memset(d_scale_table[:].bitcast(I32), 0)
+        nc.vector.memset(x_scale_table[:, : T // 2].bitcast(I32), 0)
+        nc.gpsimd.memset(x_scale_table[:, T // 2 :].bitcast(I32), 0)
+        nc.vector.memset(scales[:].bitcast(I32), 0)
+        nc.vector.memset(identity[:], 0.0)
+        make_identity(nc, identity[:], nomemset=True)
 
         nc.sync.dma_start(kidx_sb[:], kidx)
+        d_source = d_words[0].rearrange("p n t -> p (n t)").bitcast(I32)
+        nc.sync.dma_start(d_table[:, :D_AHEAD].bitcast(I32), d_source[:, :D_AHEAD])
         nc.sync.dma_start(offs_sb[:], offs)
         nc.sync.dma_start(slot_sb[:], slot)
         nc.sync.dma_start(gn_sb[:], gn.rearrange("(p t) o -> p (t o)", t=PACK))
-        nc.sync.dma_start(ds_tab[0:P:8, :].bitcast(I32), d_scales[0].bitcast(I32))
-        d_src = d_words[0].rearrange("p n t -> p (n t)").bitcast(I32)
-        nc.sync.dma_start(d_tab[:, :PIECE].bitcast(I32), d_src[:, :PIECE])
-        nc.sync.dma_start(xs_tab[0:P:8, :].bitcast(I32), x_scales[0].bitcast(I32))
-        nc.sync.dma_start(d_tab[:, PIECE:].bitcast(I32), d_src[:, PIECE:])
-        nc.sync.dma_start(x_tab[:].bitcast(I32), x_words[0].rearrange("p n t -> p (n t)").bitcast(I32))
-        load_page(ORDER[0], "page_first")
+        nc.sync.dma_start(d_scale_table[0:P:BLOCK_ROWS, :].bitcast(I32), d_scales[0].bitcast(I32))
+        nc.sync.dma_start(x_scale_table[0:P:BLOCK_ROWS, :].bitcast(I32), x_scales[0].bitcast(I32))
+        nc.sync.dma_start(d_table[:, D_AHEAD:].bitcast(I32), d_source[:, D_AHEAD:])
+        nc.sync.dma_start(x_table[:].bitcast(I32), x_words[0].rearrange("p n t -> p (n t)").bitcast(I32))
+        load_page(PLANES[0], "page_first")
 
-        sc_got = keep.tile([P, H + S], U8, name="sc_got", tag="room_c", align_bytes=64)
-        d_got = keep.tile([P, H], U32, name="d_got", tag="room_d", align_bytes=64)
-        x_got = keep.tile([P, S], U32, name="x_got", align_bytes=64)
+        scales_picked = keep.tile([P, H + S], U8, name="scales_picked", tag="scales_picked", align_bytes=64)
+        d_picked = keep.tile([P, H], U32, name="d_picked", tag="d_picked", align_bytes=64)
+        x_picked = keep.tile([P, S], U32, name="x_picked", align_bytes=64)
         held = [keep.tile([P, S], F32, name=f"held{t}") for t in range(PACK)]
 
-        def fetch_held(t):
+        nc.vector.tensor_copy(scales_picked[:, :H], d_scale_table[:].indirect(kidx_sb[:]))
+        nc.vector.tensor_copy(scales_picked[:, H:], x_scale_table[:].indirect(offs_sb[:]))
+        for j in range(QUADRANT // BLOCK_ROWS):
+            nc.scalar.dma_start(
+                scales[j:P:QUADRANT, :].bitcast(I32), scales_picked[BLOCK_ROWS * j : P : QUADRANT, :].bitcast(I32)
+            )
+        nc.vector.tensor_copy(d_picked[:], d_table[:].indirect(kidx_sb[:]))
+        load_page(PLANES[1], "d_table")
+        load_page(PLANES[2], "scales_picked")
+        nc.vector.tensor_copy(x_picked[:], x_table[:].indirect(offs_sb[:]))
+        load_page(PLANES[3], "x_table")
+        for t in PLANES:
             nc.vector.tensor_copy(held[t][:], page[t][:].indirect(slot_sb[:]))
 
-        nc.vector.tensor_copy(sc_got[:, :H], ds_tab[:].indirect(kidx_sb[:]))
-        nc.vector.tensor_copy(sc_got[:, H:], xs_tab[:].indirect(offs_sb[:]))
-        for j in range(4):
-            nc.scalar.dma_start(planes[j:P:32, :].bitcast(I32), sc_got[8 * j : P : 32, :].bitcast(I32))
-        nc.vector.tensor_copy(d_got[:], d_tab[:].indirect(kidx_sb[:]))
-        load_page(ORDER[1], "room_a")
-        load_page(ORDER[2], "room_c")
-        nc.vector.tensor_copy(x_got[:], x_tab[:].indirect(offs_sb[:]))
-        load_page(ORDER[3], "room_b")
-        for t in ORDER:
-            fetch_held(t)
-
-        raw = []
+        token_scores = []
         for b in range(S // P):
-            bank = psum.tile([P, H], F32, name=f"raw{b}", tag="bank")
-            cols = slice(b * P, (b + 1) * P)
+            bank = psum.tile([P, H], F32, name=f"token_scores{b}", tag="bank")
             nc.tensor.matmul_mx(
                 out=bank[:],
-                lhsT=x_got[:, cols].bitcast(FP8X4),
-                lhsT_scale=planes[:, H + b * P : H + (b + 1) * P],
-                rhs=d_got[:].bitcast(FP8X4),
-                rhs_scale=planes[:, :H],
+                lhsT=x_picked[:, b * P : (b + 1) * P].bitcast(FP8X4),
+                lhsT_scale=scales[:, H + b * P : H + (b + 1) * P],
+                rhs=d_picked[:].bitcast(FP8X4),
+                rhs_scale=scales[:, :H],
                 start=True,
                 stop=True,
             )
-            raw.append(bank[:].rearrange("p (m t) -> p t m", t=PACK))
-        w_raw = keep.tile([P, PACK, N], F32, name="w_raw", tag="room_d", align_bytes=64)
+            token_scores.append(bank[:].rearrange("p (m t) -> p t m", t=PACK))
+        w_raw = keep.tile([P, PACK, N], F32, name="w_raw", tag="d_picked", align_bytes=64)
         nc.sync.dma_start(w_raw[:], w1.rearrange("(p t) n -> p t n", t=PACK))
-        dealt = [keep.tile([P, PACK, P], F32, name=f"dealt{b}") for b in range(S // P)]
-        score = {t: psum.tile([P, S], F32, name=f"score{t}", tag="bank") for t in ORDER}
-
-        def turn(t):
-            for b in range(S // P):
-                nc.tensor.transpose(score[t][:, b * P : (b + 1) * P], dealt[b][:, t, :], ident[:])
-
+        by_plane = [keep.tile([P, PACK, P], F32, name=f"by_plane{b}") for b in range(S // P)]
+        score = {t: psum.tile([P, S], F32, name=f"score{t}", tag="bank") for t in PLANES}
         for b in range(S // P):
-            nc.scalar.activation(dealt[b][:], raw[b], COPY, scale=0.0625)
-        for t in ORDER:
-            turn(t)
+            nc.scalar.activation(by_plane[b][:], token_scores[b], COPY, scale=SCORE_SCALE)
+        for t in PLANES:
+            for b in range(S // P):
+                nc.tensor.transpose(score[t][:, b * P : (b + 1) * P], by_plane[b][:, t, :], identity[:])
 
-        starts = [sum(CHUNKS[:c]) for c in range(len(CHUNKS))]
-        z = [keep.tile([P, w, PACK], BF16, name=f"z{c}", tag=f"room_z{c}", align_bytes=64) for c, w in enumerate(CHUNKS)]
+        z = [keep.tile([P, CHUNK, PACK], BF16, name=f"z{c}", tag=f"z{c}", align_bytes=64) for c in range(CHUNKS)]
         w_bf = keep.tile([P, N, PACK], BF16, name="w_bf", align_bytes=64)
-        w_sc = keep.tile([P, N], U8, name="w_sc", align_bytes=64)
-
+        w_scales = keep.tile([P, N], U8, name="w_scales", align_bytes=64)
         new = {}
 
         def take_larger(t):
-            new[t] = keep.tile([P, S], F32, name=f"new{t}", tag=f"room_new{t}", align_bytes=64)
-            nc.vector.scalar_tensor_tensor(new[t][:], held[t][:], 0.5, score[t][:], ALU.mult, ALU.max)
+            new[t] = keep.tile([P, S], F32, name=f"new{t}", tag=f"new{t}", align_bytes=64)
+            nc.vector.scalar_tensor_tensor(new[t][:], held[t][:], OLD_SCALE, score[t][:], ALU.mult, ALU.max)
+
+        def weigh_on_scalar(t, c, weight):
+            nc.scalar.activation(z[c][:, :, t], page[t][:, c * CHUNK : (c + 1) * CHUNK], COPY, scale=weight)
+
+        def weigh_on_vector(t, c, weight):
+            nc.vector.tensor_scalar(z[c][:, :, t], page[t][:, c * CHUNK : (c + 1) * CHUNK], weight, None, ALU.mult)
 
         nc.scalar.copy(w_bf[:], w_raw[:].rearrange("p t n -> p n t"))
-        gn_use = keep.tile([P, PACK], F32, name="gn_use", tag="room_d", align_bytes=64)
-        nc.scalar.copy(gn_use[:], gn_sb[:])
-        take_larger(ORDER[0])
-        for i, t in enumerate(ORDER):
-            if i + 1 < PACK:
-                take_larger(ORDER[i + 1])
+        gn_scalar = keep.tile([P, PACK], F32, name="gn_scalar", tag="d_picked", align_bytes=64)
+        nc.scalar.copy(gn_scalar[:], gn_sb[:])
+
+        last = PLANES[-1]
+        take_larger(PLANES[0])
+        for i, t in enumerate(PLANES):
+            if t != last:
+                take_larger(PLANES[i + 1])
             nc.vector.tensor_copy(page[t][:].indirect(slot_sb[:]), new[t][:])
-            if i + 1 < PACK:
-                for c, w in enumerate(CHUNKS):
-                    nc.scalar.activation(
-                        z[c][:, :, t], page[t][:, starts[c] : starts[c] + w], COPY, scale=gn_use[:, t : t + 1]
-                    )
+            if t != last:
+                for c in range(CHUNKS):
+                    weigh_on_scalar(t, c, gn_scalar[:, t : t + 1])
 
-        t = ORDER[-1]
-        z_codes = [keep.tile([P, w], U32, name=f"z_codes{c}", align_bytes=64) for c, w in enumerate(CHUNKS)]
-        z_sc = [keep.tile([P, w], U8, name=f"z_sc{c}", align_bytes=64) for c, w in enumerate(CHUNKS)]
-
-        def weigh_last(c, weight):
-            cols = slice(starts[c], starts[c] + CHUNKS[c])
-            if c in SCALAR_CHUNKS:
-                nc.scalar.activation(z[c][:, :, t], page[t][:, cols], COPY, scale=weight)
-            else:
-                nc.vector.tensor_scalar(z[c][:, :, t], page[t][:, cols], weight, None, ALU.mult)
+        z_codes = [keep.tile([P, CHUNK], U32, name=f"z_codes{c}", align_bytes=64) for c in range(CHUNKS)]
+        z_scales = [keep.tile([P, CHUNK], U8, name=f"z_scales{c}", align_bytes=64) for c in range(CHUNKS)]
 
         def quantise_z(c):
             nc.vector.quantize_mx(
-                out=z_codes[c][:].bitcast(FP8X4), scales=z_sc[c][:], in_=z[c][:].rearrange("p n t -> p (n t)")
+                out=z_codes[c][:].bitcast(FP8X4), scales=z_scales[c][:], in_=z[c][:].rearrange("p n t -> p (n t)")
             )
 
-        def multiply(c, m0, per_bank, on_vector):
-            w = CHUNKS[c]
-            acc = psum.tile([P, per_bank, w], F32, name=f"acc{c}_{m0}", tag="bank")
-            for a in range(per_bank):
-                cols = slice((m0 + a) * P, (m0 + a + 1) * P)
+        weigh_on_scalar(last, 0, gn_scalar[:, last : last + 1])
+        weigh_on_scalar(last, 1, gn_scalar[:, last : last + 1])
+        w_codes = keep.tile([P, N], U32, name="w_codes", tag=f"new{last}", align_bytes=64)
+        nc.vector.quantize_mx(
+            out=w_codes[:].bitcast(FP8X4), scales=w_scales[:], in_=w_bf[:].rearrange("p n t -> p (n t)")
+        )
+        quantise_z(0)
+        gn_vector = keep.tile([P, 1], F32, name="gn_vector", tag="z0", align_bytes=64)
+        nc.vector.tensor_copy(gn_vector[:], gn_sb[:, last : last + 1])
+        weigh_on_vector(last, 2, gn_vector[:])
+        quantise_z(1)
+        weigh_on_vector(last, 3, gn_vector[:])
+        quantise_z(2)
+        quantise_z(3)
+
+        def multiply(c, first, blocks, copy_out):
+            acc = psum.tile([P, blocks, CHUNK], F32, name=f"acc{c}_{first}", tag="bank")
+            for a in range(blocks):
+                w_cols = slice((first + a) * P, (first + a + 1) * P)
                 nc.tensor.matmul_mx(
                     out=acc[:, a, :],
-                    lhsT=w_codes[:, cols].bitcast(FP8X4),
-                    lhsT_scale=w_sc[:, cols],
+                    lhsT=w_codes[:, w_cols].bitcast(FP8X4),
+                    lhsT_scale=w_scales[:, w_cols],
                     rhs=z_codes[c][:].bitcast(FP8X4),
-                    rhs_scale=z_sc[c][:],
+                    rhs_scale=z_scales[c][:],
                     start=True,
                     stop=True,
                 )
-            res = keep.tile([P, per_bank, w], F32, name=f"res{c}_{m0}")
-            if on_vector:
-                nc.vector.tensor_copy(res[:], acc[:])
-            else:
-                nc.scalar.copy(res[:], acc[:])
-            nc.sync.dma_start(
-                out[m0 * P : (m0 + per_bank) * P, starts[c] : starts[c] + w].rearrange("(a p) n -> p a n", p=P),
-                res[:],
-            )
+            result = keep.tile([P, blocks, CHUNK], F32, name=f"result{c}_{first}")
+            copy_out(result[:], acc[:])
+            rows = out[first * P : (first + blocks) * P, c * CHUNK : (c + 1) * CHUNK]
+            nc.sync.dma_start(rows.rearrange("(a p) n -> p a n", p=P), result[:])
 
-        weigh_last(0, gn_use[:, t : t + 1])
-        weigh_last(1, gn_use[:, t : t + 1])
-        w_codes = keep.tile([P, N], U32, name="w_codes", tag=f"room_new{t}", align_bytes=64)
-        nc.vector.quantize_mx(out=w_codes[:].bitcast(FP8X4), scales=w_sc[:], in_=w_bf[:].rearrange("p n t -> p (n t)"))
-        quantise_z(0)
-        gn_last = keep.tile([P, 1], F32, name="gn_last", tag="room_z0", align_bytes=64)
-        nc.vector.tensor_copy(gn_last[:], gn_sb[:, t : t + 1])
-        weigh_last(2, gn_last[:])
-        quantise_z(1)
-        weigh_last(3, gn_last[:])
-        quantise_z(2)
-        quantise_z(3)
-        multiply(0, 0, 1, False)
-        multiply(0, 1, 1, False)
-        multiply(0, 2, 2, False)
-        for c in (1, 2, 3):
-            multiply(c, 0, 2, False)
-            multiply(c, 2, 2, c >= 2)
+        multiply(0, 0, 1, nc.scalar.copy)
+        multiply(0, 1, 1, nc.scalar.copy)
+        multiply(0, 2, 2, nc.scalar.copy)
+        multiply(1, 0, 2, nc.scalar.copy)
+        multiply(1, 2, 2, nc.scalar.copy)
+        for c in (2, 3):
+            multiply(c, 0, 2, nc.scalar.copy)
+            multiply(c, 2, 2, nc.vector.tensor_copy)

from contextlib import ExitStack

import concourse.mybir as mybir
from concourse.masks import make_identity

K, T, S, N, G, H, U = 512, 2048, 512, 512, 2048, 512, 1024
FLOPS = 2 * K * H * S + 2 * H * N * U

F32 = mybir.dt.float32
BF16 = mybir.dt.bfloat16
I32 = mybir.dt.int32
U32 = mybir.dt.uint32
U16 = mybir.dt.uint16
U8 = mybir.dt.uint8
FP8X4 = mybir.dt.float8_e4m3fn_x4
ALU = mybir.AluOpType
COPY = mybir.ActivationFunctionType.Copy

P = 128
PACK = 4
GROUP = 16
BLOCK_ROWS = 8
QUADRANT = 32
PSUM_BANKS = 8
SCORE_SCALE = 0.0625
OLD_SCALE = 0.5

PLANES = (0, 2, 3, 1)
CHUNK = 256
CHUNKS = U // CHUNK
D_AHEAD = 512


def tile_picked_scorepage_none_p_kernel(
    tc, x_words, x_scales, d_words, d_scales, old, gn, w1, offs, kidx, slot, out
):
    nc = tc.nc
    with ExitStack() as ctx:
        keep = ctx.enter_context(tc.tile_pool(name="keep", bufs=1))
        psum = ctx.enter_context(tc.psum_pool(name="psum", bufs=PSUM_BANKS))

        kidx_sb = keep.tile([P, H // GROUP], U16, name="kidx_sb")
        offs_sb = keep.tile([P, S // GROUP], U16, name="offs_sb")
        slot_sb = keep.tile([P, S // GROUP], U16, name="slot_sb")
        gn_sb = keep.tile([P, PACK], F32, name="gn_sb")
        d_table = keep.tile([P, G], U32, name="d_table", tag="d_table", align_bytes=64)
        x_table = keep.tile([P, T], U32, name="x_table", tag="x_table", align_bytes=64)
        d_scale_table = keep.tile([P, G], U8, name="d_scale_table", align_bytes=64)
        x_scale_table = keep.tile([P, T], U8, name="x_scale_table", align_bytes=64)
        scales = keep.tile([P, H + S], U8, name="scales", align_bytes=64)
        identity = keep.tile([P, P], F32, name="identity")
        page = {}
        old_planes = old.rearrange("(p t) u -> t p u", t=PACK)

        def load_page(t, tag):
            page[t] = keep.tile([P, U], F32, name=f"page{t}", tag=tag, align_bytes=64)
            nc.sync.dma_start(page[t][:], old_planes[t])

        nc.vector.memset(d_scale_table[:].bitcast(I32), 0)
        nc.vector.memset(x_scale_table[:, : T // 2].bitcast(I32), 0)
        nc.gpsimd.memset(x_scale_table[:, T // 2 :].bitcast(I32), 0)
        nc.vector.memset(scales[:].bitcast(I32), 0)
        nc.vector.memset(identity[:], 0.0)
        make_identity(nc, identity[:], nomemset=True)

        nc.sync.dma_start(kidx_sb[:], kidx)
        d_source = d_words[0].rearrange("p n t -> p (n t)").bitcast(I32)
        nc.sync.dma_start(d_table[:, :D_AHEAD].bitcast(I32), d_source[:, :D_AHEAD])
        nc.sync.dma_start(offs_sb[:], offs)
        nc.sync.dma_start(slot_sb[:], slot)
        nc.sync.dma_start(gn_sb[:], gn.rearrange("(p t) o -> p (t o)", t=PACK))
        nc.sync.dma_start(d_scale_table[0:P:BLOCK_ROWS, :].bitcast(I32), d_scales[0].bitcast(I32))
        nc.sync.dma_start(x_scale_table[0:P:BLOCK_ROWS, :].bitcast(I32), x_scales[0].bitcast(I32))
        nc.sync.dma_start(d_table[:, D_AHEAD:].bitcast(I32), d_source[:, D_AHEAD:])
        nc.sync.dma_start(x_table[:].bitcast(I32), x_words[0].rearrange("p n t -> p (n t)").bitcast(I32))
        load_page(PLANES[0], "page_first")

        scales_picked = keep.tile([P, H + S], U8, name="scales_picked", tag="scales_picked", align_bytes=64)
        d_picked = keep.tile([P, H], U32, name="d_picked", tag="d_picked", align_bytes=64)
        x_picked = keep.tile([P, S], U32, name="x_picked", align_bytes=64)
        held = [keep.tile([P, S], F32, name=f"held{t}") for t in range(PACK)]

        nc.vector.tensor_copy(scales_picked[:, :H], d_scale_table[:].indirect(kidx_sb[:]))
        nc.vector.tensor_copy(scales_picked[:, H:], x_scale_table[:].indirect(offs_sb[:]))
        for j in range(QUADRANT // BLOCK_ROWS):
            nc.scalar.dma_start(
                scales[j:P:QUADRANT, :].bitcast(I32), scales_picked[BLOCK_ROWS * j : P : QUADRANT, :].bitcast(I32)
            )
        nc.vector.tensor_copy(d_picked[:], d_table[:].indirect(kidx_sb[:]))
        load_page(PLANES[1], "d_table")
        load_page(PLANES[2], "scales_picked")
        nc.vector.tensor_copy(x_picked[:], x_table[:].indirect(offs_sb[:]))
        load_page(PLANES[3], "x_table")
        for t in PLANES:
            nc.vector.tensor_copy(held[t][:], page[t][:].indirect(slot_sb[:]))

        token_scores = []
        for b in range(S // P):
            bank = psum.tile([P, H], F32, name=f"token_scores{b}", tag="bank")
            nc.tensor.matmul_mx(
                out=bank[:],
                lhsT=x_picked[:, b * P : (b + 1) * P].bitcast(FP8X4),
                lhsT_scale=scales[:, H + b * P : H + (b + 1) * P],
                rhs=d_picked[:].bitcast(FP8X4),
                rhs_scale=scales[:, :H],
                start=True,
                stop=True,
            )
            token_scores.append(bank[:].rearrange("p (m t) -> p t m", t=PACK))
        w_raw = keep.tile([P, PACK, N], F32, name="w_raw", tag="d_picked", align_bytes=64)
        nc.sync.dma_start(w_raw[:], w1.rearrange("(p t) n -> p t n", t=PACK))
        by_plane = [keep.tile([P, PACK, P], F32, name=f"by_plane{b}") for b in range(S // P)]
        score = {t: psum.tile([P, S], F32, name=f"score{t}", tag="bank") for t in PLANES}
        for b in range(S // P):
            nc.scalar.activation(by_plane[b][:], token_scores[b], COPY, scale=SCORE_SCALE)
        for t in PLANES:
            for b in range(S // P):
                nc.tensor.transpose(score[t][:, b * P : (b + 1) * P], by_plane[b][:, t, :], identity[:])

        z = [keep.tile([P, CHUNK, PACK], BF16, name=f"z{c}", tag=f"z{c}", align_bytes=64) for c in range(CHUNKS)]
        w_bf = keep.tile([P, N, PACK], BF16, name="w_bf", align_bytes=64)
        w_scales = keep.tile([P, N], U8, name="w_scales", align_bytes=64)
        new = {}

        def take_larger(t):
            new[t] = keep.tile([P, S], F32, name=f"new{t}", tag=f"new{t}", align_bytes=64)
            nc.vector.scalar_tensor_tensor(new[t][:], held[t][:], OLD_SCALE, score[t][:], ALU.mult, ALU.max)

        def weigh_on_scalar(t, c, weight):
            nc.scalar.activation(z[c][:, :, t], page[t][:, c * CHUNK : (c + 1) * CHUNK], COPY, scale=weight)

        def weigh_on_vector(t, c, weight):
            nc.vector.tensor_scalar(z[c][:, :, t], page[t][:, c * CHUNK : (c + 1) * CHUNK], weight, None, ALU.mult)

        nc.scalar.copy(w_bf[:], w_raw[:].rearrange("p t n -> p n t"))
        gn_scalar = keep.tile([P, PACK], F32, name="gn_scalar", tag="d_picked", align_bytes=64)
        nc.scalar.copy(gn_scalar[:], gn_sb[:])

        last = PLANES[-1]
        take_larger(PLANES[0])
        for i, t in enumerate(PLANES):
            if t != last:
                take_larger(PLANES[i + 1])
            nc.vector.tensor_copy(page[t][:].indirect(slot_sb[:]), new[t][:])
            if t != last:
                for c in range(CHUNKS):
                    weigh_on_scalar(t, c, gn_scalar[:, t : t + 1])

        z_codes = [keep.tile([P, CHUNK], U32, name=f"z_codes{c}", align_bytes=64) for c in range(CHUNKS)]
        z_scales = [keep.tile([P, CHUNK], U8, name=f"z_scales{c}", align_bytes=64) for c in range(CHUNKS)]

        def quantise_z(c):
            nc.vector.quantize_mx(
                out=z_codes[c][:].bitcast(FP8X4), scales=z_scales[c][:], in_=z[c][:].rearrange("p n t -> p (n t)")
            )

        weigh_on_scalar(last, 0, gn_scalar[:, last : last + 1])
        weigh_on_scalar(last, 1, gn_scalar[:, last : last + 1])
        w_codes = keep.tile([P, N], U32, name="w_codes", tag=f"new{last}", align_bytes=64)
        nc.vector.quantize_mx(
            out=w_codes[:].bitcast(FP8X4), scales=w_scales[:], in_=w_bf[:].rearrange("p n t -> p (n t)")
        )
        quantise_z(0)
        gn_vector = keep.tile([P, 1], F32, name="gn_vector", tag="z0", align_bytes=64)
        nc.vector.tensor_copy(gn_vector[:], gn_sb[:, last : last + 1])
        weigh_on_vector(last, 2, gn_vector[:])
        quantise_z(1)
        weigh_on_vector(last, 3, gn_vector[:])
        quantise_z(2)
        quantise_z(3)

        def multiply(c, first, blocks, copy_out):
            acc = psum.tile([P, blocks, CHUNK], F32, name=f"acc{c}_{first}", tag="bank")
            for a in range(blocks):
                w_cols = slice((first + a) * P, (first + a + 1) * P)
                nc.tensor.matmul_mx(
                    out=acc[:, a, :],
                    lhsT=w_codes[:, w_cols].bitcast(FP8X4),
                    lhsT_scale=w_scales[:, w_cols],
                    rhs=z_codes[c][:].bitcast(FP8X4),
                    rhs_scale=z_scales[c][:],
                    start=True,
                    stop=True,
                )
            result = keep.tile([P, blocks, CHUNK], F32, name=f"result{c}_{first}")
            copy_out(result[:], acc[:])
            rows = out[first * P : (first + blocks) * P, c * CHUNK : (c + 1) * CHUNK]
            nc.sync.dma_start(rows.rearrange("(a p) n -> p a n", p=P), result[:])

        multiply(0, 0, 1, nc.scalar.copy)
        multiply(0, 1, 1, nc.scalar.copy)
        multiply(0, 2, 2, nc.scalar.copy)
        multiply(1, 0, 2, nc.scalar.copy)
        multiply(1, 2, 2, nc.scalar.copy)
        for c in (2, 3):
            multiply(c, 0, 2, nc.scalar.copy)
            multiply(c, 2, 2, nc.vector.tensor_copy)
